import numpy as np
import ml_dtypes


def mxq(x, axis, fmt="e4m3"):
    dtype, down = {"e4m3": (ml_dtypes.float8_e4m3fn, 7), "e5m2": (ml_dtypes.float8_e5m2, 14)}[fmt]
    v = np.moveaxis(np.asarray(x, np.float32).astype(ml_dtypes.bfloat16).astype(np.float64), axis, -1)
    blocks = v.reshape(v.shape[:-1] + (-1, 32))
    amax = np.abs(blocks).max(-1, keepdims=True)
    byte = np.maximum(np.where(amax > 0, np.frexp(amax)[1] - 1 + 127, 0) - down, 1)
    scale = np.exp2(byte - 127.0)
    codes = (blocks / scale).astype(np.float32).astype(dtype).astype(np.float64)
    return np.moveaxis((codes * scale).reshape(v.shape), -1, axis)


WIDE = False


def mx_kscale(k):
    if not WIDE:
        return np.ones(k)
    levels = np.array([10, -10, 5, -5, 0])
    if k % 512:
        return np.exp2(np.random.permutation(np.resize(levels, k // 32))).repeat(32)
    a = np.empty((k // 512, 16))
    for p in range(k // 512):
        a[p, :8] = np.random.permutation(np.resize(levels, 8))
        for g in range(8):
            far = levels[np.abs(levels - a[p, g]) >= 10]
            a[p, g + 8] = far[np.random.randint(len(far))]
    return np.exp2(a.ravel()).repeat(32)


def f64(x):
    return np.asarray(x).astype(np.float64)


def striped(idx):
    return np.tile(np.asarray(idx).reshape(-1, 16).T, (8, 1)).astype(np.uint16)


def unstriped(offs):
    return offs[:16].T.reshape(-1).astype(np.int64)


def striped8(idx):
    return np.asarray(idx).reshape(8, -1, 16).transpose(0, 2, 1).reshape(128, -1).astype(np.uint16)


def unstriped8(offs):
    return offs.reshape(8, 16, -1).transpose(0, 2, 1).reshape(8, -1).astype(np.int64)


def pick8(x, idx, run):
    r = np.arange(len(x))
    return x[r[:, None], idx[r % (8 * run) // run]]


E2M1 = np.array([0.0, 0.5, 1.0, 1.5, 2.0, 3.0, 4.0, 6.0, -0.0, -0.5, -1.0, -1.5, -2.0, -3.0, -4.0, -6.0])


def pack_weight(w, fmt):
    k, n = w.shape
    w = f64(np.asarray(w, np.float32).astype(ml_dtypes.bfloat16)).reshape(k // 32, 32, n)
    amax = np.abs(w).max(1)
    if fmt == "e4m3":
        byte = np.frexp(amax)[1] - 1 + 127 - 7
    else:
        mant, ex = np.frexp(amax / 6.0)
        byte = np.where(mant > 0.5, ex, ex - 1) + 127
    byte = np.clip(np.where(amax > 0, byte, 1), 1, 254)
    scaled = (w * np.exp2(127.0 - byte)[:, None, :]).reshape(k, n).astype(np.float32)
    by_word = np.ascontiguousarray(scaled.reshape(k // 512, 128, 4, n).transpose(0, 1, 3, 2))
    if fmt == "e4m3":
        words = by_word.astype(ml_dtypes.float8_e4m3fn).view(np.uint8)
    else:
        c = by_word.astype(ml_dtypes.float4_e2m1fn).view(np.uint8) & 0xF
        words = (c[..., 0::2] | (c[..., 1::2] << 4)).reshape(k // 512, 128, 2 * n)
    return np.ascontiguousarray(words), np.ascontiguousarray(byte.astype(np.uint8).reshape(k // 512, 16, n))


def unpack_weight(words, scales, fmt):
    g, _, n = scales.shape
    words = np.ascontiguousarray(words).reshape(g, 128, n, -1)
    if fmt == "e4m3":
        vals = words.view(ml_dtypes.float8_e4m3fn).astype(np.float64)
    else:
        nib = np.empty((g, 128, n, 4), np.uint8)
        nib[..., 0::2] = words & 0xF
        nib[..., 1::2] = words >> 4
        vals = E2M1[nib]
    vals = vals * np.repeat(np.exp2(scales.astype(np.float64) - 127.0), 8, axis=1)[..., None]
    return vals.transpose(0, 1, 3, 2).reshape(g * 512, n)


K, J, R, T, F, O, N, U = 512, 512, 512, 1024, 1024, 256, 256, 128


def setup_inputs():
    n = np.random.standard_normal
    idx = np.stack([np.random.permutation(T)[:J] for _ in range(8)])
    idx2 = np.stack([np.random.permutation(T)[:J] for _ in range(8)])
    idx3 = np.stack([np.random.permutation(F)[:R] for _ in range(8)])
    idx4 = np.random.permutation(J)[:O]
    idx5 = np.stack([np.random.permutation(J)[:O] for _ in range(8)])
    idx6 = np.stack([np.random.permutation(O)[:U] for _ in range(8)])
    idx7 = np.stack([np.random.permutation(O)[:U] for _ in range(8)])
    fk = mx_kscale(K)
    fr = mx_kscale(R)
    wbp = pack_weight(n((R, N)) * 1 / np.sqrt(R) / fr[:, None], "e4m3")
    wop = pack_weight(n((R, N)) * 1 / np.sqrt(R) / fr[:, None], "e2m1")
    return {
        "ta": (np.random.randint(-7, 8, (K, T)).astype(np.float64)).astype(np.float32),
        "ga": ((np.random.randint(10, 25, (K, 1)) / 64.0) * fk[:, None]).astype(np.float32),
        "gb": ((np.random.randint(4, 13, (K, 1)) / 64.0) * fk[:, None]).astype(np.float32),
        "ua": (np.random.randint(-7, 8, (K, F)).astype(np.float64)).astype(np.float32),
        "ha": ((np.random.randint(8, 25, (K, 1)) / 1024.0) / fk[:, None]).astype(np.float32),
        "sa": (np.random.uniform(0.5, 1.6, (R, 1)) * fr[:, None]).astype(np.float32),
        "sb": (np.random.uniform(0.5, 1.6, (R, 1)) * fr[:, None]).astype(np.float32),
        "wb_words": wbp[0],
        "wb_scales": wbp[1],
        "wo_words": wop[0],
        "wo_scales": wop[1],
        "so": (np.random.uniform(0.5, 1.6, (N, 1))).astype(np.float32),
        "sp": (np.random.uniform(0.5, 1.6, (N, 1))).astype(np.float32),
        "offs": striped8(idx),
        "offs2": striped8(idx2),
        "offs3": striped8(idx3),
        "offs4": striped(idx4),
        "offs5": striped8(idx5),
        "offs6": striped8(idx6),
        "offs7": striped8(idx7),
    }


def reference(ta, ga, gb, ua, ha, sa, sb, wb_words, wb_scales, wo_words, wo_scales, so, sp, offs, offs2, offs3, offs4, offs5, offs6, offs7):
    idx = unstriped8(offs)
    idx2 = unstriped8(offs2)
    idx3 = unstriped8(offs3)
    idx4 = unstriped(offs4)
    idx5 = unstriped8(offs5)
    idx6 = unstriped8(offs6)
    idx7 = unstriped8(offs7)
    wbu = unpack_weight(wb_words, wb_scales, "e4m3")
    wou = unpack_weight(wo_words, wo_scales, "e2m1")
    xc = pick8(f64(ta), idx, 64) * f64(ga) + pick8(f64(ta), idx2, 64) * f64(gb)
    wc = pick8(f64(ua), idx3, 64) * f64(ha)
    wcq = mxq(wc, 0, "e4m3")
    xcq = mxq(xc, 0, "e4m3")
    a = wcq.T @ xcq
    hid = np.maximum(a[:, idx4] * f64(sa), pick8(a, idx5, 64) * f64(sb))
    hidq = mxq(hid, 0, "e4m3")
    p = wbu.T @ hidq
    q = wou.T @ hidq
    y = pick8(p, idx6, 16) * f64(so) - pick8(q, idx7, 16) * f64(sp)
    return y

@@ -1,0 +1,200 @@
+from contextlib import ExitStack
+
+import concourse.mybir as mybir
+
+K, J, R, T, O, N, U = 512, 512, 512, 1024, 256, 256, 128
+FLOPS = 2 * K * R * J + 2 * 2 * R * N * O
+
+F32 = mybir.dt.float32
+BF16 = mybir.dt.bfloat16
+I32 = mybir.dt.int32
+U32 = mybir.dt.uint32
+U16 = mybir.dt.uint16
+U8 = mybir.dt.uint8
+FP8X4 = mybir.dt.float8_e4m3fn_x4
+FP4X4 = mybir.dt.float4_e2m1fn_x4
+COPY = mybir.ActivationFunctionType.Copy
+ALU = mybir.AluOpType
+
+P = 128
+PACK = 4
+STRIPE = 16
+
+
+def tile_picked_refined_codes_one_mixedpair_outcomes_outmeet_kernel(
+    tc, ta, ga, gb, ua, ha, sa, sb, wb_words, wb_scales, wo_words, wo_scales, so, sp,
+    offs, offs2, offs3, offs4, offs5, offs6, offs7, out,
+):
+    nc = tc.nc
+    with ExitStack() as ctx:
+        keep = ctx.enter_context(tc.tile_pool(name="keep", bufs=1))
+        psum = ctx.enter_context(tc.psum_pool(name="psum", bufs=1))
+
+        def load_list(src, name):
+            t = keep.tile(list(src.shape), U16, name=name)
+            nc.sync.dma_start(t[:], src)
+            return t
+
+        def load_dealt(src, name, queue):
+            t = keep.tile([P, PACK], F32, name=name)
+            queue.dma_start(t[:], src.rearrange("(p t) o -> p (t o)", t=PACK))
+            return t
+
+        def load_rows(src, plane, name):
+            t = keep.tile([P, T], F32, name=name)
+            nc.sync.dma_start(t[:], src.rearrange("(p t) c -> p t c", t=PACK)[:, plane, :])
+            return t
+
+        def fetch(dst, window, lst, first, count, scale):
+            nc.scalar.activation(
+                out=dst,
+                in_=window[:].indirect(lst[:, first // STRIPE : (first + count) // STRIPE]),
+                func=COPY,
+                scale=scale,
+            )
+
+        ga_t = load_dealt(ga, "ga_t", nc.scalar)
+        gb_t = load_dealt(gb, "gb_t", nc.scalar)
+        ta_t = [load_rows(ta, 0, "ta0")]
+        l1 = load_list(offs, "l1")
+        l2 = load_list(offs2, "l2")
+        for j in range(1, PACK):
+            ta_t.append(load_rows(ta, j, "ta%d" % j))
+        l3 = load_list(offs3, "l3")
+        ha_t = load_dealt(ha, "ha_t", nc.sync)
+        ua_t = [load_rows(ua, j, "ua%d" % j) for j in range(PACK)]
+        l4 = load_list(offs4, "l4")
+        l5 = load_list(offs5, "l5")
+        sa_t = load_dealt(sa, "sa_t", nc.sync)
+        sb_t = load_dealt(sb, "sb_t", nc.sync)
+        wb_codes = keep.tile([P, N], U32, align_bytes=64)
+        nc.sync.dma_start(wb_codes[:].bitcast(I32), wb_words[0].rearrange("p n t -> p (n t)").bitcast(I32))
+        wo_codes = keep.tile([P, 2 * N], U8, align_bytes=64)
+        nc.sync.dma_start(wo_codes[:].bitcast(I32), wo_words[0].bitcast(I32))
+        wb_plane = keep.tile([P, N], U8, align_bytes=64)
+        wo_plane = keep.tile([P, N], U8, align_bytes=64)
+        for plane, src in ((wb_plane, wb_scales), (wo_plane, wo_scales)):
+            nc.vector.memset(plane[:].bitcast(U32), 0)
+            for q in range(4):
+                nc.sync.dma_start(plane[32 * q : 32 * q + 4, :].bitcast(I32), src[0, 4 * q : 4 * q + 4, :].bitcast(I32))
+        l6 = load_list(offs6, "l6")
+        l7 = load_list(offs7, "l7")
+        so_t = keep.tile([P, N // P], F32)
+        sp_t = keep.tile([P, N // P], F32)
+        with nc.allow_non_contiguous_dma(reason="one value a partition and output tile"):
+            nc.sync.dma_start(so_t[:], so.rearrange("(i p) o -> p (i o)", p=P))
+            nc.sync.dma_start(sp_t[:], sp.rearrange("(i p) o -> p (i o)", p=P))
+
+        x_planes = keep.tile([P, PACK, J], BF16)
+        for j in range(PACK):
+            coarse = keep.tile([P, J], F32, name="coarse%d" % j)
+            fine = keep.tile([P, J], F32, name="fine%d" % j)
+            fetch(coarse[:], ta_t[j], l1, 0, J, ga_t[:, j : j + 1])
+            fetch(fine[:], ta_t[j], l2, 0, J, gb_t[:, j : j + 1])
+            nc.vector.tensor_tensor(x_planes[:, j, :], coarse[:], fine[:], ALU.add)
+        x_woven = keep.tile([P, J * PACK], BF16, align_bytes=64)
+        nc.vector.tensor_copy(
+            x_woven[:].rearrange("p (c i t) -> p c t i", i=4, t=PACK),
+            x_planes[:].rearrange("p t (c i) -> p c t i", i=4),
+        )
+        x_codes = keep.tile([P, J], U32, align_bytes=64)
+        x_plane = keep.tile([P, J], U8, align_bytes=64)
+        nc.vector.quantize_mx(out=x_codes[:].bitcast(FP8X4), scales=x_plane[:], in_=x_woven[:])
+
+        HALF = R // 2
+        w_half = [keep.tile([P, PACK, HALF], BF16, name="w_half%d" % h) for h in range(2)]
+        w_woven = [keep.tile([P, P * PACK], BF16, name="w_woven%d" % t, align_bytes=64) for t in range(PACK)]
+        w_codes = [keep.tile([P, P], U32, name="w_codes%d" % t, align_bytes=64) for t in range(PACK)]
+        w_plane = [keep.tile([P, P], U8, name="w_plane%d" % t, align_bytes=64) for t in range(PACK)]
+
+        def weave_w(h, t):
+            nc.vector.tensor_copy(
+                w_woven[t][:, h * HALF : (h + 1) * HALF].rearrange("p (m j) -> p m j", j=PACK),
+                w_half[h][:].rearrange("p j (m t) -> p t m j", t=PACK)[:, t],
+            )
+
+        def quantise_w(t):
+            nc.vector.quantize_mx(out=w_codes[t][:].bitcast(FP8X4), scales=w_plane[t][:], in_=w_woven[t][:])
+
+        for h in range(2):
+            for j in range(PACK):
+                fetch(w_half[h][:, j, :], ua_t[j], l3, h * HALF, HALF, ha_t[:, j : j + 1])
+        for t in range(PACK):
+            weave_w(0, t)
+        weave_w(1, 0)
+        for t in range(1, PACK):
+            weave_w(1, t)
+            quantise_w(t - 1)
+        quantise_w(PACK - 1)
+
+        a_t = [keep.tile([P, J], F32, name="a%d" % t) for t in range(PACK)]
+
+        def first_product(t, first, count, bank, engine_copy):
+            acc = psum.tile([P, count], F32, name="acc_a%d_%d" % (t, first), tag="bank%d" % bank)
+            nc.tensor.matmul_mx(
+                out=acc[:], lhsT=w_codes[t][:].bitcast(FP8X4), lhsT_scale=w_plane[t][:],
+                rhs=x_codes[:, first : first + count].bitcast(FP8X4), rhs_scale=x_plane[:, first : first + count],
+                start=True, stop=True,
+            )
+            engine_copy(a_t[t][:, first : first + count], acc[:])
+
+        first_product(0, 0, J // 2, 0, nc.scalar.copy)
+        first_product(0, J // 2, J // 2, 1, nc.scalar.copy)
+        for t in range(1, PACK):
+            first_product(t, 0, J, 1 + t, nc.vector.tensor_copy)
+
+        OH = O // 2
+        shared = [keep.tile([P, PACK, OH], F32, name="shared%d" % h) for h in range(2)]
+        own = [keep.tile([P, PACK, OH], F32, name="own%d" % h) for h in range(2)]
+        for t, h in [(0, 0), (0, 1), (1, 0), (2, 0), (3, 0), (1, 1), (2, 1), (3, 1)]:
+            fetch(shared[h][:, t, :], a_t[t], l4, h * OH, OH, sa_t[:, t : t + 1])
+            fetch(own[h][:, t, :], a_t[t], l5, h * OH, OH, sb_t[:, t : t + 1])
+
+        h_codes = [keep.tile([P, OH], U32, name="h_codes%d" % h, align_bytes=64) for h in range(2)]
+        h_plane = [keep.tile([P, OH], U8, name="h_plane%d" % h, align_bytes=64) for h in range(2)]
+        for h in range(2):
+            h_woven = keep.tile([P, OH * PACK], BF16, name="h_woven%d" % h, align_bytes=64)
+            nc.vector.tensor_tensor(
+                h_woven[:].rearrange("p (c i t) -> p c t i", i=4, t=PACK),
+                shared[h][:].rearrange("p t (c i) -> p c t i", i=4),
+                own[h][:].rearrange("p t (c i) -> p c t i", i=4),
+                ALU.max,
+            )
+            nc.vector.quantize_mx(out=h_codes[h][:].bitcast(FP8X4), scales=h_plane[h][:], in_=h_woven[:])
+
+        outcome = [[keep.tile([P, O], F32, name="outcome%d_%d" % (i, m)) for m in range(2)] for i in range(N // P)]
+
+        def second_product(acc, i, m, h):
+            if m == 0:
+                codes = wb_codes[:, i * P : (i + 1) * P].bitcast(FP8X4)
+                plane = wb_plane[:, i * P : (i + 1) * P]
+            else:
+                codes = wo_codes[:, 2 * i * P : 2 * (i + 1) * P].bitcast(FP4X4)
+                plane = wo_plane[:, i * P : (i + 1) * P]
+            nc.tensor.matmul_mx(
+                out=acc, lhsT=codes, lhsT_scale=plane,
+                rhs=h_codes[h][:].bitcast(FP8X4), rhs_scale=h_plane[h][:], start=True, stop=True,
+            )
+
+        pairs = [(i, m) for i in range(N // P) for m in range(2)]
+        early = psum.tile([P, len(pairs), OH], F32, tag="bank5")
+        for s, (i, m) in enumerate(pairs):
+            second_product(early[:, s, :], i, m, 0)
+        for s, (i, m) in enumerate(pairs):
+            nc.vector.tensor_copy(outcome[i][m][:, 0:OH], early[:, s, :])
+        for s, (i, m) in enumerate(pairs):
+            late = psum.tile([P, OH], F32, name="late%d" % s, tag="bank%d" % ((6 + s) % 8))
+            second_product(late[:], i, m, 1)
+            if s == 0:
+                nc.scalar.copy(outcome[i][m][:, OH:O], late[:])
+            else:
+                nc.vector.tensor_copy(outcome[i][m][:, OH:O], late[:])
+
+        for i in range(N // P):
+            first = keep.tile([P, U], F32, name="first%d" % i)
+            second = keep.tile([P, U], F32, name="second%d" % i)
+            result = keep.tile([P, U], F32, name="result%d" % i)
+            fetch(first[:], outcome[i][0], l6, 0, U, so_t[:, i : i + 1])
+            fetch(second[:], outcome[i][1], l7, 0, U, sp_t[:, i : i + 1])
+            nc.vector.tensor_tensor(result[:], first[:], second[:], ALU.subtract)
+            nc.sync.dma_start(out[i * P : (i + 1) * P, :], result[:])

@@ -53,9 +53,13 @@ def tile_picked_refined_codes_one_mixedpair_outcomes_outmeet_kernel(
                 scale=scale,
             )
 
+        ta_t = [load_rows(ta, 0, "ta0")]
         ga_t = load_dealt(ga, "ga_t", nc.scalar)
         gb_t = load_dealt(gb, "gb_t", nc.scalar)
-        ta_t = [load_rows(ta, 0, "ta0")]
+        warm_in = keep.tile([P, 8], F32)
+        warm_out = keep.tile([P, 8], F32)
+        nc.vector.memset(warm_in[:], 0.0)
+        nc.scalar.activation(out=warm_out[:], in_=warm_in[:], func=COPY)
         l1 = load_list(offs, "l1")
         l2 = load_list(offs2, "l2")
         for j in range(1, PACK):
@@ -101,31 +105,17 @@ def tile_picked_refined_codes_one_mixedpair_outcomes_outmeet_kernel(
         x_plane = keep.tile([P, J], U8, align_bytes=64)
         nc.vector.quantize_mx(out=x_codes[:].bitcast(FP8X4), scales=x_plane[:], in_=x_woven[:])
 
-        HALF = R // 2
-        w_half = [keep.tile([P, PACK, HALF], BF16, name="w_half%d" % h) for h in range(2)]
-        w_woven = [keep.tile([P, P * PACK], BF16, name="w_woven%d" % t, align_bytes=64) for t in range(PACK)]
+        w_planes = keep.tile([P, PACK, R], BF16)
+        w_woven = [keep.tile([P, P, PACK], BF16, name="w_woven%d" % t, align_bytes=64) for t in range(PACK)]
         w_codes = [keep.tile([P, P], U32, name="w_codes%d" % t, align_bytes=64) for t in range(PACK)]
         w_plane = [keep.tile([P, P], U8, name="w_plane%d" % t, align_bytes=64) for t in range(PACK)]
-
-        def weave_w(h, t):
-            nc.vector.tensor_copy(
-                w_woven[t][:, h * HALF : (h + 1) * HALF].rearrange("p (m j) -> p m j", j=PACK),
-                w_half[h][:].rearrange("p j (m t) -> p t m j", t=PACK)[:, t],
-            )
-
-        def quantise_w(t):
-            nc.vector.quantize_mx(out=w_codes[t][:].bitcast(FP8X4), scales=w_plane[t][:], in_=w_woven[t][:])
-
-        for h in range(2):
-            for j in range(PACK):
-                fetch(w_half[h][:, j, :], ua_t[j], l3, h * HALF, HALF, ha_t[:, j : j + 1])
+        for j in range(PACK):
+            fetch(w_planes[:, j, :], ua_t[j], l3, 0, R, ha_t[:, j : j + 1])
         for t in range(PACK):
-            weave_w(0, t)
-        weave_w(1, 0)
-        for t in range(1, PACK):
-            weave_w(1, t)
-            quantise_w(t - 1)
-        quantise_w(PACK - 1)
+            nc.vector.tensor_copy(w_woven[t][:], w_planes[:].rearrange("p j (m t) -> p t m j", t=PACK)[:, t])
+            nc.vector.quantize_mx(
+                out=w_codes[t][:].bitcast(FP8X4), scales=w_plane[t][:], in_=w_woven[t][:].rearrange("p m j -> p (m j)")
+            )
 
         a_t = [keep.tile([P, J], F32, name="a%d" % t) for t in range(PACK)]
 
@@ -141,30 +131,52 @@ def tile_picked_refined_codes_one_mixedpair_outcomes_outmeet_kernel(
         first_product(0, 0, J // 2, 0, nc.scalar.copy)
         first_product(0, J // 2, J // 2, 1, nc.scalar.copy)
         for t in range(1, PACK):
-            first_product(t, 0, J, 1 + t, nc.vector.tensor_copy)
+            for h in range(2):
+                first_product(t, h * J // 2, J // 2, 2 * t + h, nc.vector.tensor_copy)
 
         OH = O // 2
-        shared = [keep.tile([P, PACK, OH], F32, name="shared%d" % h) for h in range(2)]
-        own = [keep.tile([P, PACK, OH], F32, name="own%d" % h) for h in range(2)]
-        for t, h in [(0, 0), (0, 1), (1, 0), (2, 0), (3, 0), (1, 1), (2, 1), (3, 1)]:
-            fetch(shared[h][:, t, :], a_t[t], l4, h * OH, OH, sa_t[:, t : t + 1])
-            fetch(own[h][:, t, :], a_t[t], l5, h * OH, OH, sb_t[:, t : t + 1])
-
-        h_codes = [keep.tile([P, OH], U32, name="h_codes%d" % h, align_bytes=64) for h in range(2)]
-        h_plane = [keep.tile([P, OH], U8, name="h_plane%d" % h, align_bytes=64) for h in range(2)]
+        OQ = O // 4
+        LAST = PACK - 1
+        shared = keep.tile([P, LAST, O], F32)
+        own = keep.tile([P, LAST, O], F32)
+        for t in range(LAST):
+            fetch(shared[:, t, :], a_t[t], l4, 0, O, sa_t[:, t : t + 1])
+            fetch(own[:, t, :], a_t[t], l5, 0, O, sb_t[:, t : t + 1])
+        pieces = [(0, OH), (OH, OQ), (OH + OQ, OQ)]
+        shared_last = [keep.tile([P, count], F32, name="shared_last%d" % first) for first, count in pieces]
+        own_last = [keep.tile([P, OH], F32, name="own_last%d" % h) for h in range(2)]
+        fetch(shared_last[0][:], a_t[LAST], l4, 0, OH, sa_t[:, LAST:PACK])
         for h in range(2):
-            h_woven = keep.tile([P, OH * PACK], BF16, name="h_woven%d" % h, align_bytes=64)
+            fetch(own_last[h][:], a_t[LAST], l5, h * OH, OH, sb_t[:, LAST:PACK])
+        for e in range(1, len(pieces)):
+            fetch(shared_last[e][:], a_t[LAST], l4, pieces[e][0], pieces[e][1], sa_t[:, LAST:PACK])
+
+        h_codes = keep.tile([P, O], U32, align_bytes=64)
+        h_plane = keep.tile([P, O], U8, align_bytes=64)
+        h_woven = [keep.tile([P, OH, PACK], BF16, name="h_woven%d" % h, align_bytes=64) for h in range(2)]
+        for h in range(2):
             nc.vector.tensor_tensor(
-                h_woven[:].rearrange("p (c i t) -> p c t i", i=4, t=PACK),
-                shared[h][:].rearrange("p t (c i) -> p c t i", i=4),
-                own[h][:].rearrange("p t (c i) -> p c t i", i=4),
+                h_woven[h][:].rearrange("p (c i) t -> p c t i", i=4)[:, :, 0:LAST, :],
+                shared[:, :, h * OH : (h + 1) * OH].rearrange("p t (c i) -> p c t i", i=4),
+                own[:, :, h * OH : (h + 1) * OH].rearrange("p t (c i) -> p c t i", i=4),
                 ALU.max,
             )
-            nc.vector.quantize_mx(out=h_codes[h][:].bitcast(FP8X4), scales=h_plane[h][:], in_=h_woven[:])
+        for e, (first, count) in enumerate(pieces):
+            h, at = divmod(first, OH)
+            nc.vector.tensor_tensor(
+                h_woven[h][:, at : at + count, LAST], shared_last[e][:], own_last[h][:, at : at + count], ALU.max
+            )
+        for h in range(2):
+            nc.vector.quantize_mx(
+                out=h_codes[:, h * OH : (h + 1) * OH].bitcast(FP8X4),
+                scales=h_plane[:, h * OH : (h + 1) * OH],
+                in_=h_woven[h][:].rearrange("p o t -> p (o t)"),
+            )
 
         outcome = [[keep.tile([P, O], F32, name="outcome%d_%d" % (i, m)) for m in range(2)] for i in range(N // P)]
 
-        def second_product(acc, i, m, h):
+        def second_product(i, m, first, count, bank, engine_copy):
+            acc = psum.tile([P, count], F32, name="acc_o%d_%d_%d" % (i, m, first), tag="bank%d" % bank)
             if m == 0:
                 codes = wb_codes[:, i * P : (i + 1) * P].bitcast(FP8X4)
                 plane = wb_plane[:, i * P : (i + 1) * P]
@@ -172,23 +184,17 @@ def tile_picked_refined_codes_one_mixedpair_outcomes_outmeet_kernel(
                 codes = wo_codes[:, 2 * i * P : 2 * (i + 1) * P].bitcast(FP4X4)
                 plane = wo_plane[:, i * P : (i + 1) * P]
             nc.tensor.matmul_mx(
-                out=acc, lhsT=codes, lhsT_scale=plane,
-                rhs=h_codes[h][:].bitcast(FP8X4), rhs_scale=h_plane[h][:], start=True, stop=True,
+                out=acc[:], lhsT=codes, lhsT_scale=plane,
+                rhs=h_codes[:, first : first + count].bitcast(FP8X4), rhs_scale=h_plane[:, first : first + count],
+                start=True, stop=True,
             )
+            engine_copy(outcome[i][m][:, first : first + count], acc[:])
 
-        pairs = [(i, m) for i in range(N // P) for m in range(2)]
-        early = psum.tile([P, len(pairs), OH], F32, tag="bank5")
-        for s, (i, m) in enumerate(pairs):
-            second_product(early[:, s, :], i, m, 0)
-        for s, (i, m) in enumerate(pairs):
-            nc.vector.tensor_copy(outcome[i][m][:, 0:OH], early[:, s, :])
-        for s, (i, m) in enumerate(pairs):
-            late = psum.tile([P, OH], F32, name="late%d" % s, tag="bank%d" % ((6 + s) % 8))
-            second_product(late[:], i, m, 1)
-            if s == 0:
-                nc.scalar.copy(outcome[i][m][:, OH:O], late[:])
-            else:
-                nc.vector.tensor_copy(outcome[i][m][:, OH:O], late[:])
+        for h in range(2):
+            second_product(0, 0, h * OH, OH, 2 * h, nc.scalar.copy)
+            second_product(0, 1, h * OH, OH, 2 * h + 1, nc.vector.tensor_copy)
+        second_product(1, 0, 0, O, 4, nc.vector.tensor_copy)
+        second_product(1, 1, 0, O, 5, nc.vector.tensor_copy)
 
         for i in range(N // P):
             first = keep.tile([P, U], F32, name="first%d" % i)

from contextlib import ExitStack

import concourse.mybir as mybir

K, J, R, T, O, N, U = 512, 512, 512, 1024, 256, 256, 128
FLOPS = 2 * K * R * J + 2 * 2 * R * N * O

F32 = mybir.dt.float32
BF16 = mybir.dt.bfloat16
I32 = mybir.dt.int32
U32 = mybir.dt.uint32
U16 = mybir.dt.uint16
U8 = mybir.dt.uint8
FP8X4 = mybir.dt.float8_e4m3fn_x4
FP4X4 = mybir.dt.float4_e2m1fn_x4
COPY = mybir.ActivationFunctionType.Copy
ALU = mybir.AluOpType

P = 128
PACK = 4
STRIPE = 16


def tile_picked_refined_codes_one_mixedpair_outcomes_outmeet_kernel(
    tc, ta, ga, gb, ua, ha, sa, sb, wb_words, wb_scales, wo_words, wo_scales, so, sp,
    offs, offs2, offs3, offs4, offs5, offs6, offs7, out,
):
    nc = tc.nc
    with ExitStack() as ctx:
        keep = ctx.enter_context(tc.tile_pool(name="keep", bufs=1))
        psum = ctx.enter_context(tc.psum_pool(name="psum", bufs=1))

        def load_list(src, name):
            t = keep.tile(list(src.shape), U16, name=name)
            nc.sync.dma_start(t[:], src)
            return t

        def load_dealt(src, name, queue):
            t = keep.tile([P, PACK], F32, name=name)
            queue.dma_start(t[:], src.rearrange("(p t) o -> p (t o)", t=PACK))
            return t

        def load_rows(src, plane, name):
            t = keep.tile([P, T], F32, name=name)
            nc.sync.dma_start(t[:], src.rearrange("(p t) c -> p t c", t=PACK)[:, plane, :])
            return t

        def fetch(dst, window, lst, first, count, scale):
            nc.scalar.activation(
                out=dst,
                in_=window[:].indirect(lst[:, first // STRIPE : (first + count) // STRIPE]),
                func=COPY,
                scale=scale,
            )

        ta_t = [load_rows(ta, 0, "ta0")]
        ga_t = load_dealt(ga, "ga_t", nc.scalar)
        gb_t = load_dealt(gb, "gb_t", nc.scalar)
        warm_in = keep.tile([P, 8], F32)
        warm_out = keep.tile([P, 8], F32)
        nc.vector.memset(warm_in[:], 0.0)
        nc.scalar.activation(out=warm_out[:], in_=warm_in[:], func=COPY)
        l1 = load_list(offs, "l1")
        l2 = load_list(offs2, "l2")
        for j in range(1, PACK):
            ta_t.append(load_rows(ta, j, "ta%d" % j))
        l3 = load_list(offs3, "l3")
        ha_t = load_dealt(ha, "ha_t", nc.sync)
        ua_t = [load_rows(ua, j, "ua%d" % j) for j in range(PACK)]
        l4 = load_list(offs4, "l4")
        l5 = load_list(offs5, "l5")
        sa_t = load_dealt(sa, "sa_t", nc.sync)
        sb_t = load_dealt(sb, "sb_t", nc.sync)
        wb_codes = keep.tile([P, N], U32, align_bytes=64)
        nc.sync.dma_start(wb_codes[:].bitcast(I32), wb_words[0].rearrange("p n t -> p (n t)").bitcast(I32))
        wo_codes = keep.tile([P, 2 * N], U8, align_bytes=64)
        nc.sync.dma_start(wo_codes[:].bitcast(I32), wo_words[0].bitcast(I32))
        wb_plane = keep.tile([P, N], U8, align_bytes=64)
        wo_plane = keep.tile([P, N], U8, align_bytes=64)
        for plane, src in ((wb_plane, wb_scales), (wo_plane, wo_scales)):
            nc.vector.memset(plane[:].bitcast(U32), 0)
            for q in range(4):
                nc.sync.dma_start(plane[32 * q : 32 * q + 4, :].bitcast(I32), src[0, 4 * q : 4 * q + 4, :].bitcast(I32))
        l6 = load_list(offs6, "l6")
        l7 = load_list(offs7, "l7")
        so_t = keep.tile([P, N // P], F32)
        sp_t = keep.tile([P, N // P], F32)
        with nc.allow_non_contiguous_dma(reason="one value a partition and output tile"):
            nc.sync.dma_start(so_t[:], so.rearrange("(i p) o -> p (i o)", p=P))
            nc.sync.dma_start(sp_t[:], sp.rearrange("(i p) o -> p (i o)", p=P))

        x_planes = keep.tile([P, PACK, J], BF16)
        for j in range(PACK):
            coarse = keep.tile([P, J], F32, name="coarse%d" % j)
            fine = keep.tile([P, J], F32, name="fine%d" % j)
            fetch(coarse[:], ta_t[j], l1, 0, J, ga_t[:, j : j + 1])
            fetch(fine[:], ta_t[j], l2, 0, J, gb_t[:, j : j + 1])
            nc.vector.tensor_tensor(x_planes[:, j, :], coarse[:], fine[:], ALU.add)
        x_woven = keep.tile([P, J * PACK], BF16, align_bytes=64)
        nc.vector.tensor_copy(
            x_woven[:].rearrange("p (c i t) -> p c t i", i=4, t=PACK),
            x_planes[:].rearrange("p t (c i) -> p c t i", i=4),
        )
        x_codes = keep.tile([P, J], U32, align_bytes=64)
        x_plane = keep.tile([P, J], U8, align_bytes=64)
        nc.vector.quantize_mx(out=x_codes[:].bitcast(FP8X4), scales=x_plane[:], in_=x_woven[:])

        w_planes = keep.tile([P, PACK, R], BF16)
        w_woven = [keep.tile([P, P, PACK], BF16, name="w_woven%d" % t, align_bytes=64) for t in range(PACK)]
        w_codes = [keep.tile([P, P], U32, name="w_codes%d" % t, align_bytes=64) for t in range(PACK)]
        w_plane = [keep.tile([P, P], U8, name="w_plane%d" % t, align_bytes=64) for t in range(PACK)]
        for j in range(PACK):
            fetch(w_planes[:, j, :], ua_t[j], l3, 0, R, ha_t[:, j : j + 1])
        for t in range(PACK):
            nc.vector.tensor_copy(w_woven[t][:], w_planes[:].rearrange("p j (m t) -> p t m j", t=PACK)[:, t])
            nc.vector.quantize_mx(
                out=w_codes[t][:].bitcast(FP8X4), scales=w_plane[t][:], in_=w_woven[t][:].rearrange("p m j -> p (m j)")
            )

        a_t = [keep.tile([P, J], F32, name="a%d" % t) for t in range(PACK)]

        def first_product(t, first, count, bank, engine_copy):
            acc = psum.tile([P, count], F32, name="acc_a%d_%d" % (t, first), tag="bank%d" % bank)
            nc.tensor.matmul_mx(
                out=acc[:], lhsT=w_codes[t][:].bitcast(FP8X4), lhsT_scale=w_plane[t][:],
                rhs=x_codes[:, first : first + count].bitcast(FP8X4), rhs_scale=x_plane[:, first : first + count],
                start=True, stop=True,
            )
            engine_copy(a_t[t][:, first : first + count], acc[:])

        first_product(0, 0, J // 2, 0, nc.scalar.copy)
        first_product(0, J // 2, J // 2, 1, nc.scalar.copy)
        for t in range(1, PACK):
            for h in range(2):
                first_product(t, h * J // 2, J // 2, 2 * t + h, nc.vector.tensor_copy)

        OH = O // 2
        OQ = O // 4
        LAST = PACK - 1
        shared = keep.tile([P, LAST, O], F32)
        own = keep.tile([P, LAST, O], F32)
        for t in range(LAST):
            fetch(shared[:, t, :], a_t[t], l4, 0, O, sa_t[:, t : t + 1])
            fetch(own[:, t, :], a_t[t], l5, 0, O, sb_t[:, t : t + 1])
        pieces = [(0, OH), (OH, OQ), (OH + OQ, OQ)]
        shared_last = [keep.tile([P, count], F32, name="shared_last%d" % first) for first, count in pieces]
        own_last = [keep.tile([P, OH], F32, name="own_last%d" % h) for h in range(2)]
        fetch(shared_last[0][:], a_t[LAST], l4, 0, OH, sa_t[:, LAST:PACK])
        for h in range(2):
            fetch(own_last[h][:], a_t[LAST], l5, h * OH, OH, sb_t[:, LAST:PACK])
        for e in range(1, len(pieces)):
            fetch(shared_last[e][:], a_t[LAST], l4, pieces[e][0], pieces[e][1], sa_t[:, LAST:PACK])

        h_codes = keep.tile([P, O], U32, align_bytes=64)
        h_plane = keep.tile([P, O], U8, align_bytes=64)
        h_woven = [keep.tile([P, OH, PACK], BF16, name="h_woven%d" % h, align_bytes=64) for h in range(2)]
        for h in range(2):
            nc.vector.tensor_tensor(
                h_woven[h][:].rearrange("p (c i) t -> p c t i", i=4)[:, :, 0:LAST, :],
                shared[:, :, h * OH : (h + 1) * OH].rearrange("p t (c i) -> p c t i", i=4),
                own[:, :, h * OH : (h + 1) * OH].rearrange("p t (c i) -> p c t i", i=4),
                ALU.max,
            )
        for e, (first, count) in enumerate(pieces):
            h, at = divmod(first, OH)
            nc.vector.tensor_tensor(
                h_woven[h][:, at : at + count, LAST], shared_last[e][:], own_last[h][:, at : at + count], ALU.max
            )
        for h in range(2):
            nc.vector.quantize_mx(
                out=h_codes[:, h * OH : (h + 1) * OH].bitcast(FP8X4),
                scales=h_plane[:, h * OH : (h + 1) * OH],
                in_=h_woven[h][:].rearrange("p o t -> p (o t)"),
            )

        outcome = [[keep.tile([P, O], F32, name="outcome%d_%d" % (i, m)) for m in range(2)] for i in range(N // P)]

        def second_product(i, m, first, count, bank, engine_copy):
            acc = psum.tile([P, count], F32, name="acc_o%d_%d_%d" % (i, m, first), tag="bank%d" % bank)
            if m == 0:
                codes = wb_codes[:, i * P : (i + 1) * P].bitcast(FP8X4)
                plane = wb_plane[:, i * P : (i + 1) * P]
            else:
                codes = wo_codes[:, 2 * i * P : 2 * (i + 1) * P].bitcast(FP4X4)
                plane = wo_plane[:, i * P : (i + 1) * P]
            nc.tensor.matmul_mx(
                out=acc[:], lhsT=codes, lhsT_scale=plane,
                rhs=h_codes[:, first : first + count].bitcast(FP8X4), rhs_scale=h_plane[:, first : first + count],
                start=True, stop=True,
            )
            engine_copy(outcome[i][m][:, first : first + count], acc[:])

        for h in range(2):
            second_product(0, 0, h * OH, OH, 2 * h, nc.scalar.copy)
            second_product(0, 1, h * OH, OH, 2 * h + 1, nc.vector.tensor_copy)
        second_product(1, 0, 0, O, 4, nc.vector.tensor_copy)
        second_product(1, 1, 0, O, 5, nc.vector.tensor_copy)

        for i in range(N // P):
            first = keep.tile([P, U], F32, name="first%d" % i)
            second = keep.tile([P, U], F32, name="second%d" % i)
            result = keep.tile([P, U], F32, name="result%d" % i)
            fetch(first[:], outcome[i][0], l6, 0, U, so_t[:, i : i + 1])
            fetch(second[:], outcome[i][1], l7, 0, U, sp_t[:, i : i + 1])
            nc.vector.tensor_tensor(result[:], first[:], second[:], ALU.subtract)
            nc.sync.dma_start(out[i * P : (i + 1) * P, :], result[:])
